import numpy as np
import ml_dtypes


def mxq(x, axis, fmt="e4m3"):
    dtype, down = {"e4m3": (ml_dtypes.float8_e4m3fn, 7), "e5m2": (ml_dtypes.float8_e5m2, 14)}[fmt]
    v = np.moveaxis(np.asarray(x, np.float32).astype(ml_dtypes.bfloat16).astype(np.float64), axis, -1)
    blocks = v.reshape(v.shape[:-1] + (-1, 32))
    amax = np.abs(blocks).max(-1, keepdims=True)
    byte = np.maximum(np.where(amax > 0, np.frexp(amax)[1] - 1 + 127, 0) - down, 1)
    scale = np.exp2(byte - 127.0)
    codes = (blocks / scale).astype(np.float32).astype(dtype).astype(np.float64)
    return np.moveaxis((codes * scale).reshape(v.shape), -1, axis)


WIDE = False


def mx_kscale(k):
    if not WIDE:
        return np.ones(k)
    levels = np.array([10, -10, 5, -5, 0])
    if k % 512:
        return np.exp2(np.random.permutation(np.resize(levels, k // 32))).repeat(32)
    a = np.empty((k // 512, 16))
    for p in range(k // 512):
        a[p, :8] = np.random.permutation(np.resize(levels, 8))
        for g in range(8):
            far = levels[np.abs(levels - a[p, g]) >= 10]
            a[p, g + 8] = far[np.random.randint(len(far))]
    return np.exp2(a.ravel()).repeat(32)


def f64(x):
    return np.asarray(x).astype(np.float64)


def striped8(idx):
    return np.asarray(idx).reshape(8, -1, 16).transpose(0, 2, 1).reshape(128, -1).astype(np.uint16)


def unstriped8(offs):
    return offs.reshape(8, 16, -1).transpose(0, 2, 1).reshape(8, -1).astype(np.int64)


def pick8(x, idx, run):
    r = np.arange(len(x))
    return x[r[:, None], idx[r % (8 * run) // run]]


E2M1 = np.array([0.0, 0.5, 1.0, 1.5, 2.0, 3.0, 4.0, 6.0, -0.0, -0.5, -1.0, -1.5, -2.0, -3.0, -4.0, -6.0])


def pack_weight(w, fmt):
    k, n = w.shape
    w = f64(np.asarray(w, np.float32).astype(ml_dtypes.bfloat16)).reshape(k // 32, 32, n)
    amax = np.abs(w).max(1)
    if fmt == "e4m3":
        byte = np.frexp(amax)[1] - 1 + 127 - 7
    else:
        mant, ex = np.frexp(amax / 6.0)
        byte = np.where(mant > 0.5, ex, ex - 1) + 127
    byte = np.clip(np.where(amax > 0, byte, 1), 1, 254)
    scaled = (w * np.exp2(127.0 - byte)[:, None, :]).reshape(k, n).astype(np.float32)
    by_word = np.ascontiguousarray(scaled.reshape(k // 512, 128, 4, n).transpose(0, 1, 3, 2))
    if fmt == "e4m3":
        words = by_word.astype(ml_dtypes.float8_e4m3fn).view(np.uint8)
    else:
        c = by_word.astype(ml_dtypes.float4_e2m1fn).view(np.uint8) & 0xF
        words = (c[..., 0::2] | (c[..., 1::2] << 4)).reshape(k // 512, 128, 2 * n)
    return np.ascontiguousarray(words), np.ascontiguousarray(byte.astype(np.uint8).reshape(k // 512, 16, n))


def unpack_weight(words, scales, fmt):
    g, _, n = scales.shape
    words = np.ascontiguousarray(words).reshape(g, 128, n, -1)
    if fmt == "e4m3":
        vals = words.view(ml_dtypes.float8_e4m3fn).astype(np.float64)
    else:
        nib = np.empty((g, 128, n, 4), np.uint8)
        nib[..., 0::2] = words & 0xF
        nib[..., 1::2] = words >> 4
        vals = E2M1[nib]
    vals = vals * np.repeat(np.exp2(scales.astype(np.float64) - 127.0), 8, axis=1)[..., None]
    return vals.transpose(0, 1, 3, 2).reshape(g * 512, n)


D, E, T, Q, I = 512, 512, 1024, 128, 512


def setup_inputs():
    n = np.random.standard_normal
    idx = np.stack([np.random.permutation(T)[:I] for _ in range(8)])
    idx2 = np.stack([np.random.permutation(T)[:I] for _ in range(8)])
    fd = mx_kscale(D)
    fe = mx_kscale(E)
    keysp = pack_weight(n((D, T)) / fd[:, None], "e4m3")
    return {
        "query": (n((D, Q)) * 0.6 / np.sqrt(D) * fd[:, None]).astype(np.float32),
        "keys_words": keysp[0],
        "keys_scales": keysp[1],
        "gout": (n((E, Q)) * 1 / np.sqrt(E) * fe[:, None]).astype(np.float32),
        "vals": (n((E, T)) / fe[:, None]).astype(np.float32),
        "share": (np.random.uniform(0.4, 0.9, (Q, 1))).astype(np.float32),
        "fac": (np.random.uniform(0.5, 2.0, (1, T))).astype(np.float32),
        "base": (0.3 * n((Q, T))).astype(np.float32),
        "offs": striped8(idx),
        "offs2": striped8(idx2),
    }


def reference(query, keys_words, keys_scales, gout, vals, share, fac, base, offs, offs2):
    idx = unstriped8(offs)
    idx2 = unstriped8(offs2)
    keysu = unpack_weight(keys_words, keys_scales, "e4m3")
    queryq = mxq(f64(query), 0, "e4m3")
    a = queryq.T @ keysu
    dl = (pick8(a, idx2, 16) - pick8(a, idx, 16)) * f64(share)
    df0 = np.zeros((Q, T))
    df0[np.arange(Q)[:, None], idx[np.arange(Q) % 128 // 16]] = dl
    s = a + df0
    p = np.exp(s - np.max(s, axis=1, keepdims=True))
    z = np.sum(p, axis=1, keepdims=True)
    goutq = mxq(f64(gout), 0, "e4m3")
    valsq = mxq(f64(vals), 0, "e4m3")
    c0 = goutq.T @ valsq
    dz = np.sum(c0 * p * f64(fac) / np.square(z) * (-1.0), axis=1, keepdims=True)
    dp = c0 / z * f64(fac) + dz
    ds = dp * p
    ddl = pick8(ds, idx, 16)
    e1 = ddl * f64(share)
    s1 = np.zeros((Q, T))
    s1[np.arange(Q)[:, None], idx2[np.arange(Q) % 128 // 16]] = e1
    e2 = ddl * f64(share) * (-1.0)
    s2 = np.zeros((Q, T))
    s2[np.arange(Q)[:, None], idx[np.arange(Q) % 128 // 16]] = e2
    da = ds + s1 + s2
    hda = da * 1024.0 * 2.0 * 1024.0
    he2 = pick8(hda, idx, 16)
    he1 = pick8(hda, idx2, 16)
    hddl = he2 * (-1.0) * f64(share) + he1 * f64(share)
    s51 = np.zeros((Q, T))
    s51[np.arange(Q)[:, None], idx[np.arange(Q) % 128 // 16]] = hddl
    hds = hda + s51
    hdp = hds * p
    hdz = np.sum(hdp, axis=1, keepdims=True)
    hz = np.sum(hdp * f64(fac) * c0 / np.square(z) * (-1.0), axis=1, keepdims=True) + np.sum(hdz * (-1.0) * c0 * p * f64(fac) / np.square(np.square(z)) * (-1.0), axis=1, keepdims=True) * z * 2.0
    hp = hds * dp + hdz * (-1.0) / np.square(z) * c0 * f64(fac) + hz
    hs = hp * p
    hdl = pick8(hs, idx, 16)
    e52 = hdl * f64(share)
    s52 = np.zeros((Q, T))
    s52[np.arange(Q)[:, None], idx2[np.arange(Q) % 128 // 16]] = e52
    e53 = hdl * f64(share) * (-1.0)
    s53 = np.zeros((Q, T))
    s53[np.arange(Q)[:, None], idx[np.arange(Q) % 128 // 16]] = e53
    ha = hs + s52 + s53
    y = ha + f64(base)
    return y

@@ -1,0 +1,292 @@
+from contextlib import ExitStack
+
+import concourse.mybir as mybir
+from concourse.masks import make_identity
+
+D, E, T, Q, SLOTS = 512, 512, 1024, 128, 512
+FLOPS = 2 * D * Q * T + 2 * E * Q * T
+
+F32 = mybir.dt.float32
+BF16 = mybir.dt.bfloat16
+I32 = mybir.dt.int32
+U32 = mybir.dt.uint32
+U16 = mybir.dt.uint16
+U8 = mybir.dt.uint8
+FP8X4 = mybir.dt.float8_e4m3fn_x4
+ALU = mybir.AluOpType
+ACT = mybir.ActivationFunctionType
+AXIS_X = mybir.AxisListType.X
+
+P = 128
+PACK = 4
+BANK = 512
+HALVES = T // BANK
+BLOCKS = BANK // P
+CHUNK = 256
+PENALTY = 1024.0 * 2.0 * 1024.0
+
+
+def half_cols(h):
+    return slice(h * BANK, (h + 1) * BANK)
+
+
+def chunk_cols(c):
+    return slice(c * CHUNK, (c + 1) * CHUNK)
+
+
+def block_cols(b):
+    return slice(b * P, (b + 1) * P)
+
+
+def interleave_views(grouped, raw):
+    return (grouped.rearrange("p (c i) j -> p c j i", i=4), raw.rearrange("p j (c i) -> p c j i", i=4))
+
+
+def tile_attend_gpborrowed_heads_kernel(tc, query, keys_words, keys_scales, gout, vals, share, fac, base, offs, offs2, out):
+    nc = tc.nc
+    with ExitStack() as ctx:
+        keep = ctx.enter_context(tc.tile_pool(name="keep", bufs=1))
+        psum = ctx.enter_context(tc.psum_pool(name="psum", bufs=1))
+
+        def sb(name, cols, dtype=F32):
+            return keep.tile([P, cols], dtype, name=name, align_bytes=64)
+
+        def banks(tag, use):
+            return [psum.tile([P, BANK], F32, name=tag + str(h) + use, tag=tag + str(h)) for h in range(HALVES)]
+
+        def turned_banks(use):
+            return [psum.tile([P, CHUNK], F32, name="turned" + str(c) + use, tag="turned" + str(c)) for c in range(T // CHUNK)]
+
+        k_scales = sb("k_scales", T, U8)
+        nc.vector.memset(k_scales[:].bitcast(I32), 0)
+        fac_rows = sb("fac_rows", P)
+        nc.gpsimd.memset(fac_rows[:], 0.0)
+        ident = sb("ident", P)
+        make_identity(nc, ident[:])
+        at_first = sb("at_first", T)
+        at_second = sb("at_second", T)
+        nc.vector.memset(at_first[:], 0.0)
+        nc.vector.memset(at_second[:], 0.0)
+
+        q_raw = keep.tile([P, PACK, Q], F32, name="q_raw")
+        nc.sync.dma_start(out=q_raw[:], in_=query.rearrange("(p j) q -> p j q", j=PACK))
+        for quad in range(4):
+            nc.scalar.dma_start(out=k_scales[32 * quad : 32 * quad + 4, :].bitcast(I32),
+                                in_=keys_scales[0, 4 * quad : 4 * quad + 4, :].bitcast(I32))
+        words = keys_words[0].rearrange("p n t -> p (n t)").bitcast(I32)
+        k_words = []
+        for h in range(HALVES):
+            k_half = sb("k_words" + str(h), BANK, I32)
+            nc.sync.dma_start(out=k_half[:], in_=words[:, half_cols(h)])
+            k_words.append(k_half)
+        share_col = sb("share_col", 1)
+        nc.sync.dma_start(out=share_col[:], in_=share)
+        first = keep.tile([P, SLOTS // 16], U16, name="first")
+        nc.sync.dma_start(first[:], offs)
+        second = keep.tile([P, SLOTS // 16], U16, name="second")
+        nc.sync.dma_start(second[:], offs2)
+        g_raw = keep.tile([P, PACK, Q], F32, name="g_raw")
+        nc.sync.dma_start(out=g_raw[:], in_=gout.rearrange("(p j) q -> p j q", j=PACK))
+        v_rows = vals.rearrange("(p j) t -> p j t", j=PACK)
+        v_raw = []
+        for c in range(T // CHUNK):
+            raw = keep.tile([P, PACK, CHUNK], F32, name="v_raw" + str(c))
+            nc.sync.dma_start(out=raw[:], in_=v_rows[:, :, c * CHUNK : (c + 1) * CHUNK])
+            v_raw.append(raw)
+        nc.sync.dma_start(out=fac_rows[0 : T // P, :], in_=fac.rearrange("o (j p) -> (o j) p", p=P))
+        base_sb = sb("base_sb", T)
+        nc.sync.dma_start(out=base_sb[:], in_=base)
+
+        warm = sb("warm", 1)
+        nc.scalar.activation(out=warm[:], in_=at_first[:, 0:1], func=ACT.Exp)
+
+        def quantize(name, grouped, cols):
+            codes = sb(name + "_codes", cols, U32)
+            scales = sb(name + "_scales", cols, U8)
+            nc.vector.quantize_mx(out=codes[:].bitcast(FP8X4), scales=scales[:], in_=grouped.rearrange("p c j -> p (c j)"))
+            return codes, scales
+
+        q_grouped = keep.tile([P, Q, PACK], BF16, name="q_grouped", align_bytes=64)
+        dst, src = interleave_views(q_grouped[:], q_raw[:])
+        nc.vector.tensor_copy(out=dst, in_=src)
+        q_codes, q_scales = quantize("q", q_grouped[:], Q)
+        a_ps = turned_banks("_a")
+        a = sb("a", T)
+        share_wide = sb("share_wide", SLOTS)
+        nc.vector.tensor_scalar(out=share_wide[:], in0=at_second[:, 0:SLOTS], scalar1=share_col[:], scalar2=None, op0=ALU.add)
+        for c in range(T // CHUNK):
+            h, lo = divmod(c * CHUNK, BANK)
+            nc.tensor.matmul_mx(out=a_ps[c][:], lhsT=q_codes[:].bitcast(FP8X4), lhsT_scale=q_scales[:],
+                                rhs=k_words[h][:, lo : lo + CHUNK].bitcast(FP8X4), rhs_scale=k_scales[:, chunk_cols(c)], start=True, stop=True)
+            if c % 2 == 0:
+                nc.scalar.copy(out=a[:, chunk_cols(c)], in_=a_ps[c][:])
+            else:
+                nc.vector.tensor_copy(out=a[:, chunk_cols(c)], in_=a_ps[c][:])
+        g_grouped = keep.tile([P, Q, PACK], BF16, name="g_grouped", align_bytes=64)
+        dst, src = interleave_views(g_grouped[:], g_raw[:])
+        nc.scalar.copy(out=dst, in_=src)
+
+        own = sb("own", SLOTS)
+        gap = sb("gap", SLOTS)
+
+        def turn_into(dst_banks, addend, opens, closes):
+            for j in range(T // P):
+                c, i = divmod(j, CHUNK // P)
+                nc.tensor.matmul(dst_banks[c][:, block_cols(i)], lhsT=addend[:, block_cols(j)], rhs=ident[:],
+                                 start=opens and i == 0, stop=closes and i == CHUNK // P - 1, is_transpose=True)
+
+        def turn_back(src_banks, use):
+            back = banks("back", use)
+            for c in range(T // CHUNK):
+                staged = sb("staged" + str(c) + use, CHUNK)
+                nc.scalar.copy(out=staged[:], in_=src_banks[c][:])
+                for i in range(CHUNK // P):
+                    h, b = divmod(c * (CHUNK // P) + i, BLOCKS)
+                    nc.tensor.transpose(back[h][:, block_cols(b)], staged[:, block_cols(i)], ident[:])
+            return back
+
+        for part in range(2):
+            nc.vector.tensor_copy(out=own[:, 256 * part : 256 * part + 256], in_=a[:].indirect(first[:, 16 * part : 16 * part + 16]))
+        for part in range(2):
+            nc.vector.tensor_tensor(out=gap[:, 256 * part : 256 * part + 256], in0=a[:].indirect(second[:, 16 * part : 16 * part + 16]),
+                                    in1=own[:, 256 * part : 256 * part + 256], op=ALU.subtract)
+        g_codes, g_scales = quantize("g", g_grouped[:], Q)
+        nc.vector.tensor_tensor(out=at_first[:].indirect(first[:]), in0=gap[:], in1=share_wide[:], op=ALU.mult)
+
+        fac_ps = psum.tile([P, P], F32, name="fac_ps", tag="u0")
+        nc.tensor.transpose(fac_ps[:], fac_rows[:], ident[:])
+        fac_cols = sb("fac_cols", T // P)
+        v_grouped = [keep.tile([P, BANK, PACK], BF16, name="v_grouped" + str(h), tag="v_grouped" + str(h), align_bytes=64) for h in range(HALVES)]
+        for c in range(T // CHUNK):
+            h, lo = divmod(c * CHUNK, BANK)
+            dst, src = interleave_views(v_grouped[h][:, lo : lo + CHUNK, :], v_raw[c][:])
+            nc.scalar.copy(out=dst, in_=src)
+        nc.scalar.copy(out=fac_cols[:], in_=fac_ps[:, 0 : T // P])
+        c_ps = turned_banks("_c")
+        u_ps = banks("u", "")
+        for h in range(HALVES):
+            v_codes, v_scales = quantize("v" + str(h), v_grouped[h][:], BANK)
+            for b in range(BLOCKS):
+                c, i = divmod(h * BLOCKS + b, CHUNK // P)
+                nc.tensor.matmul_mx(out=c_ps[c][:, block_cols(i)], lhsT=v_codes[:, block_cols(b)].bitcast(FP8X4),
+                                    lhsT_scale=v_scales[:, block_cols(b)], rhs=g_codes[:].bitcast(FP8X4), rhs_scale=g_scales[:],
+                                    start=True, stop=True)
+        for j in range(T // P):
+            c, i = divmod(j, CHUNK // P)
+            h, b = divmod(j, BLOCKS)
+            u_turned = sb("u_turned" + str(j), P)
+            nc.scalar.activation(out=u_turned[:], in_=c_ps[c][:, block_cols(i)], func=ACT.Copy, scale=fac_cols[:, j : j + 1])
+            nc.tensor.transpose(u_ps[h][:, block_cols(b)], u_turned[:], ident[:])
+
+        s = keep.tile([P, T], F32, name="s", tag="v_grouped1", align_bytes=64)
+        for h in range(HALVES):
+            nc.vector.tensor_tensor(out=s[:, half_cols(h)], in0=a[:, half_cols(h)], in1=at_first[:, half_cols(h)], op=ALU.add)
+        neg_max = sb("neg_max", 1)
+        nc.vector.tensor_reduce(out=neg_max[:], in_=s[:], axis=AXIS_X, op=ALU.max, negate=True)
+        p = [keep.tile([P, BANK], F32, name="p" + str(h), tag="p" + str(h), align_bytes=64) for h in range(HALVES)]
+        z_parts = [sb("z_part" + str(h), 1) for h in range(HALVES)]
+        for h in range(HALVES):
+            nc.scalar.activation(out=p[h][:], in_=s[:, half_cols(h)], func=ACT.Exp, bias=neg_max[:], accum_out=z_parts[h][:])
+        scrap = sb("scrap", T)
+        up_parts = [sb("up_part" + str(h), 1) for h in range(HALVES)]
+        z = sb("z", 1)
+        inv_z = sb("inv_z", 1)
+        nc.vector.scalar_tensor_tensor(out=scrap[:, half_cols(0)], in0=u_ps[0][:], scalar=1.0, in1=p[0][:], op0=ALU.mult, op1=ALU.mult, accum_out=up_parts[0][:])
+        nc.vector.tensor_tensor(out=z[:], in0=z_parts[0][:], in1=z_parts[1][:], op=ALU.add)
+        nc.vector.reciprocal(out=inv_z[:], in_=z[:])
+        nc.vector.scalar_tensor_tensor(out=scrap[:, half_cols(1)], in0=u_ps[1][:], scalar=1.0, in1=p[1][:], op0=ALU.mult, op1=ALU.mult, accum_out=up_parts[1][:])
+        prob = sb("prob", T)
+        for h in range(HALVES):
+            nc.scalar.activation(out=prob[:, half_cols(h)], in_=p[h][:], func=ACT.Copy, scale=inv_z[:])
+        u_mean = sb("u_mean", 1)
+        nc.vector.tensor_scalar(out=u_mean[:], in0=up_parts[0][:], scalar1=up_parts[1][:], scalar2=inv_z[:], op0=ALU.add, op1=ALU.mult)
+        ds = sb("ds", T)
+        for h in range(HALVES):
+            nc.vector.scalar_tensor_tensor(out=ds[:, half_cols(h)], in0=u_ps[h][:], scalar=u_mean[:], in1=prob[:, half_cols(h)], op0=ALU.subtract, op1=ALU.mult)
+
+        neg_share_penalty = keep.tile([P, SLOTS], F32, name="neg_share_penalty", tag="p0", align_bytes=64)
+        nc.scalar.activation(out=neg_share_penalty[:], in_=share_wide[:], func=ACT.Copy, scale=-PENALTY)
+
+        moved = keep.tile([P, SLOTS], F32, name="moved", tag="p1", align_bytes=64)
+        nc.scalar.activation(out=moved[:], in_=gap[:], func=ACT.Copy, scale=share_col[:])
+        listed_turned, listed_back = banks("back", "_listed")
+        for k, addend in enumerate((own, moved)):
+            for b in range(BLOCKS):
+                nc.tensor.matmul(listed_turned[:, block_cols(b)], lhsT=addend[:, block_cols(b)], rhs=ident[:],
+                                 start=k == 0 and b == 0, stop=k == 1 and b == BLOCKS - 1, is_transpose=True)
+        listed_staged = sb("listed_staged", SLOTS)
+        nc.scalar.copy(out=listed_staged[:], in_=listed_turned[:])
+        for b in range(BLOCKS):
+            nc.tensor.transpose(listed_back[:, block_cols(b)], listed_staged[:, block_cols(b)], ident[:])
+        p_listed = sb("p_listed", SLOTS)
+        nc.scalar.activation(out=p_listed[:], in_=listed_back[:], func=ACT.Exp, bias=neg_max[:])
+        share_over_z = sb("share_over_z", 1)
+        nc.scalar.activation(out=share_over_z[:], in_=share_col[:], func=ACT.Copy, scale=inv_z[:])
+
+        picked = sb("picked", SLOTS)
+        nc.vector.tensor_copy(out=picked[:], in_=ds[:].indirect(first[:]))
+        turned = turned_banks("_da")
+        turn_into(turned, ds, True, False)
+        nc.vector.tensor_tensor(out=at_second[:].indirect(second[:]), in0=picked[:], in1=share_wide[:], op=ALU.mult)
+        turn_into(turned, at_second, False, True)
+        nc.vector.tensor_tensor(out=at_first[:].indirect(first[:]), in0=picked[:], in1=neg_share_penalty[:], op=ALU.mult)
+        e1 = sb("e1", SLOTS)
+        nc.scalar.activation(out=e1[:], in_=picked[:], func=ACT.Copy, scale=share_col[:])
+        partial = turn_back(turned, "_da")
+        hda = sb("hda", T)
+        for h in range(HALVES):
+            nc.vector.scalar_tensor_tensor(out=hda[:, half_cols(h)], in0=partial[h][:], scalar=PENALTY, in1=at_first[:, half_cols(h)], op0=ALU.mult, op1=ALU.add)
+
+        squares = sb("squares", 1)
+        nc.scalar.activation(out=s[:], in_=hda[:], func=ACT.Square, accum_out=squares[:])
+        neg_energy = sb("neg_energy", 1)
+        nc.scalar.activation(out=neg_energy[:], in_=squares[:], func=ACT.Copy, scale=-1.0 / PENALTY)
+        energy_term = sb("energy_term", T)
+        nc.scalar.activation(out=energy_term[:], in_=prob[:], func=ACT.Copy, scale=neg_energy[:])
+        hda_ds = sb("hda_ds", T)
+        h_parts = sb("h_parts", 2)
+        h_own = sb("h_own", SLOTS)
+        h_gap = sb("h_gap", SLOTS)
+
+        def times_ds(lo, hi):
+            nc.vector.tensor_tensor(out=hda_ds[:, lo:hi], in0=hda[:, lo:hi], in1=ds[:, lo:hi], op=ALU.mult)
+
+        times_ds(0, CHUNK)
+        nc.vector.tensor_copy(out=h_own[:], in_=hda[:].indirect(first[:]))
+        nc.vector.scalar_tensor_tensor(out=scrap[:], in0=hda[:], scalar=1.0, in1=prob[:], op0=ALU.mult, op1=ALU.mult, accum_out=h_parts[:, 0:1])
+        nc.vector.tensor_tensor(out=h_gap[:], in0=hda[:].indirect(second[:]), in1=h_own[:], op=ALU.subtract)
+        times_ds(CHUNK, 2 * CHUNK)
+        nc.vector.scalar_tensor_tensor(out=scrap[:, 0:SLOTS], in0=h_gap[:], scalar=share_over_z[:], in1=p_listed[:], op0=ALU.mult, op1=ALU.mult, accum_out=h_parts[:, 1:2])
+        times_ds(2 * CHUNK, T)
+        nc.vector.tensor_tensor(out=at_first[:].indirect(first[:]), in0=h_gap[:], in1=e1[:], op=ALU.mult)
+        neg_parts = sb("neg_parts", 2)
+        neg_h_mean = sb("neg_h_mean", 1)
+        nc.scalar.activation(out=neg_parts[:], in_=h_parts[:], func=ACT.Copy, scale=-1.0, accum_out=neg_h_mean[:])
+        mean_term = sb("mean_term", T)
+        for c in range(T // CHUNK):
+            nc.scalar.activation(out=mean_term[:, chunk_cols(c)], in_=ds[:, chunk_cols(c)], func=ACT.Copy, scale=neg_h_mean[:])
+        turned = turned_banks("_hs")
+        turn_into(turned, energy_term, True, False)
+        turn_into(turned, hda_ds, False, False)
+        turn_into(turned, mean_term, False, True)
+        partial = turn_back(turned, "_hs")
+        hs = sb("hs", T)
+        for h in range(HALVES):
+            nc.vector.tensor_tensor(out=hs[:, half_cols(h)], in0=partial[h][:], in1=at_first[:, half_cols(h)], op=ALU.add)
+
+        neg_share_wide = keep.tile([P, SLOTS], F32, name="neg_share_wide", tag="p0", align_bytes=64)
+        nc.scalar.activation(out=neg_share_wide[:], in_=share_wide[:], func=ACT.Copy, scale=-1.0)
+        turned = turned_banks("_out")
+        turn_into(turned, base_sb, True, False)
+        nc.vector.tensor_copy(out=picked[:], in_=hs[:].indirect(first[:]))
+        turn_into(turned, hs, False, False)
+        nc.vector.tensor_tensor(out=at_second[:].indirect(second[:]), in0=picked[:], in1=share_wide[:], op=ALU.mult)
+        turn_into(turned, at_second, False, True)
+        nc.vector.tensor_tensor(out=at_first[:].indirect(first[:]), in0=picked[:], in1=neg_share_wide[:], op=ALU.mult)
+        partial = turn_back(turned, "_out")
+        for c in range(T // CHUNK):
+            h, lo = divmod(c * CHUNK, BANK)
+            result = sb("result" + str(c), CHUNK)
+            nc.vector.tensor_tensor(out=result[:], in0=partial[h][:, lo : lo + CHUNK], in1=at_first[:, chunk_cols(c)], op=ALU.add)
+            queue = nc.sync if c % 2 == 0 else nc.scalar
+            queue.dma_start(out=out[:, chunk_cols(c)], in_=result[:])

@@ -58,7 +58,7 @@ def tile_attend_gpborrowed_heads_kernel(tc, query, keys_words, keys_scales, gout
             return [psum.tile([P, CHUNK], F32, name="turned" + str(c) + use, tag="turned" + str(c)) for c in range(T // CHUNK)]
 
         k_scales = sb("k_scales", T, U8)
-        nc.vector.memset(k_scales[:].bitcast(I32), 0)
+        nc.gpsimd.memset(k_scales[:].bitcast(I32), 0)
         fac_rows = sb("fac_rows", P)
         nc.gpsimd.memset(fac_rows[:], 0.0)
         ident = sb("ident", P)
@@ -76,7 +76,7 @@ def tile_attend_gpborrowed_heads_kernel(tc, query, keys_words, keys_scales, gout
         words = keys_words[0].rearrange("p n t -> p (n t)").bitcast(I32)
         k_words = []
         for h in range(HALVES):
-            k_half = sb("k_words" + str(h), BANK, I32)
+            k_half = keep.tile([P, BANK], I32, name="k_words" + str(h), tag="k_words" + str(h), align_bytes=64)
             nc.sync.dma_start(out=k_half[:], in_=words[:, half_cols(h)])
             k_words.append(k_half)
         share_col = sb("share_col", 1)
@@ -122,7 +122,7 @@ def tile_attend_gpborrowed_heads_kernel(tc, query, keys_words, keys_scales, gout
                 nc.scalar.copy(out=a[:, chunk_cols(c)], in_=a_ps[c][:])
             else:
                 nc.vector.tensor_copy(out=a[:, chunk_cols(c)], in_=a_ps[c][:])
-        g_grouped = keep.tile([P, Q, PACK], BF16, name="g_grouped", align_bytes=64)
+        g_grouped = keep.tile([P, Q, PACK], BF16, name="g_grouped", tag="k_words1", align_bytes=64)
         dst, src = interleave_views(g_grouped[:], g_raw[:])
         nc.scalar.copy(out=dst, in_=src)
 
@@ -135,11 +135,11 @@ def tile_attend_gpborrowed_heads_kernel(tc, query, keys_words, keys_scales, gout
                 nc.tensor.matmul(dst_banks[c][:, block_cols(i)], lhsT=addend[:, block_cols(j)], rhs=ident[:],
                                  start=opens and i == 0, stop=closes and i == CHUNK // P - 1, is_transpose=True)
 
-        def turn_back(src_banks, use):
+        def turn_back(src_banks, use, scale):
             back = banks("back", use)
             for c in range(T // CHUNK):
                 staged = sb("staged" + str(c) + use, CHUNK)
-                nc.scalar.copy(out=staged[:], in_=src_banks[c][:])
+                nc.scalar.activation(out=staged[:], in_=src_banks[c][:], func=ACT.Copy, scale=scale)
                 for i in range(CHUNK // P):
                     h, b = divmod(c * (CHUNK // P) + i, BLOCKS)
                     nc.tensor.transpose(back[h][:, block_cols(b)], staged[:, block_cols(i)], ident[:])
@@ -204,22 +204,20 @@ def tile_attend_gpborrowed_heads_kernel(tc, query, keys_words, keys_scales, gout
         for h in range(HALVES):
             nc.vector.scalar_tensor_tensor(out=ds[:, half_cols(h)], in0=u_ps[h][:], scalar=u_mean[:], in1=prob[:, half_cols(h)], op0=ALU.subtract, op1=ALU.mult)
 
-        neg_share_penalty = keep.tile([P, SLOTS], F32, name="neg_share_penalty", tag="p0", align_bytes=64)
-        nc.scalar.activation(out=neg_share_penalty[:], in_=share_wide[:], func=ACT.Copy, scale=-PENALTY)
-
         moved = keep.tile([P, SLOTS], F32, name="moved", tag="p1", align_bytes=64)
         nc.scalar.activation(out=moved[:], in_=gap[:], func=ACT.Copy, scale=share_col[:])
-        listed_turned, listed_back = banks("back", "_listed")
+        listed_turned = psum.tile([P, SLOTS], F32, name="listed_turned", tag="back0")
         for k, addend in enumerate((own, moved)):
             for b in range(BLOCKS):
                 nc.tensor.matmul(listed_turned[:, block_cols(b)], lhsT=addend[:, block_cols(b)], rhs=ident[:],
                                  start=k == 0 and b == 0, stop=k == 1 and b == BLOCKS - 1, is_transpose=True)
         listed_staged = sb("listed_staged", SLOTS)
         nc.scalar.copy(out=listed_staged[:], in_=listed_turned[:])
-        for b in range(BLOCKS):
-            nc.tensor.transpose(listed_back[:, block_cols(b)], listed_staged[:, block_cols(b)], ident[:])
+        listed_back = turned_banks("_listed")
         p_listed = sb("p_listed", SLOTS)
-        nc.scalar.activation(out=p_listed[:], in_=listed_back[:], func=ACT.Exp, bias=neg_max[:])
+        for b in range(BLOCKS):
+            nc.tensor.transpose(listed_back[b][:, 0:P], listed_staged[:, block_cols(b)], ident[:])
+            nc.scalar.activation(out=p_listed[:, block_cols(b)], in_=listed_back[b][:, 0:P], func=ACT.Exp, bias=neg_max[:])
         share_over_z = sb("share_over_z", 1)
         nc.scalar.activation(out=share_over_z[:], in_=share_col[:], func=ACT.Copy, scale=inv_z[:])
 
@@ -229,13 +227,13 @@ def tile_attend_gpborrowed_heads_kernel(tc, query, keys_words, keys_scales, gout
         turn_into(turned, ds, True, False)
         nc.vector.tensor_tensor(out=at_second[:].indirect(second[:]), in0=picked[:], in1=share_wide[:], op=ALU.mult)
         turn_into(turned, at_second, False, True)
-        nc.vector.tensor_tensor(out=at_first[:].indirect(first[:]), in0=picked[:], in1=neg_share_penalty[:], op=ALU.mult)
+        nc.vector.tensor_tensor(out=at_first[:].indirect(first[:]), in0=picked[:], in1=share_wide[:], op=ALU.mult)
         e1 = sb("e1", SLOTS)
         nc.scalar.activation(out=e1[:], in_=picked[:], func=ACT.Copy, scale=share_col[:])
-        partial = turn_back(turned, "_da")
+        partial = turn_back(turned, "_da", PENALTY)
         hda = sb("hda", T)
         for h in range(HALVES):
-            nc.vector.scalar_tensor_tensor(out=hda[:, half_cols(h)], in0=partial[h][:], scalar=PENALTY, in1=at_first[:, half_cols(h)], op0=ALU.mult, op1=ALU.add)
+            nc.vector.scalar_tensor_tensor(out=hda[:, half_cols(h)], in0=at_first[:, half_cols(h)], scalar=-PENALTY, in1=partial[h][:], op0=ALU.mult, op1=ALU.add)
 
         squares = sb("squares", 1)
         nc.scalar.activation(out=s[:], in_=hda[:], func=ACT.Square, accum_out=squares[:])
@@ -269,24 +267,22 @@ def tile_attend_gpborrowed_heads_kernel(tc, query, keys_words, keys_scales, gout
         turn_into(turned, energy_term, True, False)
         turn_into(turned, hda_ds, False, False)
         turn_into(turned, mean_term, False, True)
-        partial = turn_back(turned, "_hs")
+        partial = turn_back(turned, "_hs", 1.0)
         hs = sb("hs", T)
         for h in range(HALVES):
             nc.vector.tensor_tensor(out=hs[:, half_cols(h)], in0=partial[h][:], in1=at_first[:, half_cols(h)], op=ALU.add)
 
-        neg_share_wide = keep.tile([P, SLOTS], F32, name="neg_share_wide", tag="p0", align_bytes=64)
-        nc.scalar.activation(out=neg_share_wide[:], in_=share_wide[:], func=ACT.Copy, scale=-1.0)
         turned = turned_banks("_out")
-        turn_into(turned, base_sb, True, False)
         nc.vector.tensor_copy(out=picked[:], in_=hs[:].indirect(first[:]))
-        turn_into(turned, hs, False, False)
+        turn_into(turned, hs, True, False)
+        turn_into(turned, base_sb, False, False)
         nc.vector.tensor_tensor(out=at_second[:].indirect(second[:]), in0=picked[:], in1=share_wide[:], op=ALU.mult)
         turn_into(turned, at_second, False, True)
-        nc.vector.tensor_tensor(out=at_first[:].indirect(first[:]), in0=picked[:], in1=neg_share_wide[:], op=ALU.mult)
-        partial = turn_back(turned, "_out")
+        nc.vector.tensor_tensor(out=at_first[:].indirect(first[:]), in0=picked[:], in1=share_wide[:], op=ALU.mult)
+        partial = turn_back(turned, "_out", 1.0)
         for c in range(T // CHUNK):
             h, lo = divmod(c * CHUNK, BANK)
             result = sb("result" + str(c), CHUNK)
-            nc.vector.tensor_tensor(out=result[:], in0=partial[h][:, lo : lo + CHUNK], in1=at_first[:, chunk_cols(c)], op=ALU.add)
+            nc.vector.tensor_tensor(out=result[:], in0=partial[h][:, lo : lo + CHUNK], in1=at_first[:, chunk_cols(c)], op=ALU.subtract)
             queue = nc.sync if c % 2 == 0 else nc.scalar
             queue.dma_start(out=out[:, chunk_cols(c)], in_=result[:])

@@ -85,15 +85,15 @@ def tile_attend_gpborrowed_heads_kernel(tc, query, keys_words, keys_scales, gout
         nc.sync.dma_start(first[:], offs)
         second = keep.tile([P, SLOTS // 16], U16, name="second")
         nc.sync.dma_start(second[:], offs2)
+        nc.sync.dma_start(out=fac_rows[0 : T // P, :], in_=fac.rearrange("o (j p) -> (o j) p", p=P))
         g_raw = keep.tile([P, PACK, Q], F32, name="g_raw")
         nc.sync.dma_start(out=g_raw[:], in_=gout.rearrange("(p j) q -> p j q", j=PACK))
         v_rows = vals.rearrange("(p j) t -> p j t", j=PACK)
         v_raw = []
         for c in range(T // CHUNK):
-            raw = keep.tile([P, PACK, CHUNK], F32, name="v_raw" + str(c))
+            raw = keep.tile([P, PACK, CHUNK], F32, name="v_raw" + str(c), tag="v_raw" + str(c), align_bytes=64)
             nc.sync.dma_start(out=raw[:], in_=v_rows[:, :, c * CHUNK : (c + 1) * CHUNK])
             v_raw.append(raw)
-        nc.sync.dma_start(out=fac_rows[0 : T // P, :], in_=fac.rearrange("o (j p) -> (o j) p", p=P))
         base_sb = sb("base_sb", T)
         nc.sync.dma_start(out=base_sb[:], in_=base)
 
@@ -156,12 +156,12 @@ def tile_attend_gpborrowed_heads_kernel(tc, query, keys_words, keys_scales, gout
         fac_ps = psum.tile([P, P], F32, name="fac_ps", tag="u0")
         nc.tensor.transpose(fac_ps[:], fac_rows[:], ident[:])
         fac_cols = sb("fac_cols", T // P)
+        nc.scalar.copy(out=fac_cols[:], in_=fac_ps[:, 0 : T // P])
         v_grouped = [keep.tile([P, BANK, PACK], BF16, name="v_grouped" + str(h), tag="v_grouped" + str(h), align_bytes=64) for h in range(HALVES)]
         for c in range(T // CHUNK):
             h, lo = divmod(c * CHUNK, BANK)
             dst, src = interleave_views(v_grouped[h][:, lo : lo + CHUNK, :], v_raw[c][:])
             nc.scalar.copy(out=dst, in_=src)
-        nc.scalar.copy(out=fac_cols[:], in_=fac_ps[:, 0 : T // P])
         c_ps = turned_banks("_c")
         u_ps = banks("u", "")
         for h in range(HALVES):
@@ -171,12 +171,12 @@ def tile_attend_gpborrowed_heads_kernel(tc, query, keys_words, keys_scales, gout
                 nc.tensor.matmul_mx(out=c_ps[c][:, block_cols(i)], lhsT=v_codes[:, block_cols(b)].bitcast(FP8X4),
                                     lhsT_scale=v_scales[:, block_cols(b)], rhs=g_codes[:].bitcast(FP8X4), rhs_scale=g_scales[:],
                                     start=True, stop=True)
+        u_turned = keep.tile([P, T], F32, name="u_turned", tag="v_raw3", align_bytes=64)
         for j in range(T // P):
             c, i = divmod(j, CHUNK // P)
             h, b = divmod(j, BLOCKS)
-            u_turned = sb("u_turned" + str(j), P)
-            nc.scalar.activation(out=u_turned[:], in_=c_ps[c][:, block_cols(i)], func=ACT.Copy, scale=fac_cols[:, j : j + 1])
-            nc.tensor.transpose(u_ps[h][:, block_cols(b)], u_turned[:], ident[:])
+            nc.scalar.activation(out=u_turned[:, block_cols(j)], in_=c_ps[c][:, block_cols(i)], func=ACT.Copy, scale=fac_cols[:, j : j + 1])
+            nc.tensor.transpose(u_ps[h][:, block_cols(b)], u_turned[:, block_cols(j)], ident[:])
 
         s = keep.tile([P, T], F32, name="s", tag="v_grouped1", align_bytes=64)
         for h in range(HALVES):
@@ -204,23 +204,6 @@ def tile_attend_gpborrowed_heads_kernel(tc, query, keys_words, keys_scales, gout
         for h in range(HALVES):
             nc.vector.scalar_tensor_tensor(out=ds[:, half_cols(h)], in0=u_ps[h][:], scalar=u_mean[:], in1=prob[:, half_cols(h)], op0=ALU.subtract, op1=ALU.mult)
 
-        moved = keep.tile([P, SLOTS], F32, name="moved", tag="p1", align_bytes=64)
-        nc.scalar.activation(out=moved[:], in_=gap[:], func=ACT.Copy, scale=share_col[:])
-        listed_turned = psum.tile([P, SLOTS], F32, name="listed_turned", tag="back0")
-        for k, addend in enumerate((own, moved)):
-            for b in range(BLOCKS):
-                nc.tensor.matmul(listed_turned[:, block_cols(b)], lhsT=addend[:, block_cols(b)], rhs=ident[:],
-                                 start=k == 0 and b == 0, stop=k == 1 and b == BLOCKS - 1, is_transpose=True)
-        listed_staged = sb("listed_staged", SLOTS)
-        nc.scalar.copy(out=listed_staged[:], in_=listed_turned[:])
-        listed_back = turned_banks("_listed")
-        p_listed = sb("p_listed", SLOTS)
-        for b in range(BLOCKS):
-            nc.tensor.transpose(listed_back[b][:, 0:P], listed_staged[:, block_cols(b)], ident[:])
-            nc.scalar.activation(out=p_listed[:, block_cols(b)], in_=listed_back[b][:, 0:P], func=ACT.Exp, bias=neg_max[:])
-        share_over_z = sb("share_over_z", 1)
-        nc.scalar.activation(out=share_over_z[:], in_=share_col[:], func=ACT.Copy, scale=inv_z[:])
-
         picked = sb("picked", SLOTS)
         nc.vector.tensor_copy(out=picked[:], in_=ds[:].indirect(first[:]))
         turned = turned_banks("_da")
@@ -231,6 +214,21 @@ def tile_attend_gpborrowed_heads_kernel(tc, query, keys_words, keys_scales, gout
         e1 = sb("e1", SLOTS)
         nc.scalar.activation(out=e1[:], in_=picked[:], func=ACT.Copy, scale=share_col[:])
         partial = turn_back(turned, "_da", PENALTY)
+        moved = keep.tile([P, SLOTS], F32, name="moved", tag="p1", align_bytes=64)
+        nc.scalar.activation(out=moved[:], in_=gap[:], func=ACT.Identity, scale=share_col[:], bias=neg_max[:])
+        listed_turned = psum.tile([P, SLOTS], F32, name="listed_turned", tag="u1")
+        for b in range(BLOCKS):
+            for k, addend in enumerate((moved, own)):
+                nc.tensor.matmul(listed_turned[:, block_cols(b)], lhsT=addend[:, block_cols(b)], rhs=ident[:],
+                                 start=k == 0, stop=k == 1, is_transpose=True)
+        listed_staged = sb("listed_staged", SLOTS)
+        nc.scalar.activation(out=listed_staged[:], in_=listed_turned[:], func=ACT.Exp)
+        p_listed = psum.tile([P, SLOTS], F32, name="p_listed", tag="u0")
+        for b in range(BLOCKS):
+            nc.tensor.transpose(p_listed[:, block_cols(b)], listed_staged[:, block_cols(b)], ident[:])
+        share_over_z = sb("share_over_z", 1)
+        nc.scalar.activation(out=share_over_z[:], in_=share_col[:], func=ACT.Copy, scale=inv_z[:])
+
         hda = sb("hda", T)
         for h in range(HALVES):
             nc.vector.scalar_tensor_tensor(out=hda[:, half_cols(h)], in0=at_first[:, half_cols(h)], scalar=-PENALTY, in1=partial[h][:], op0=ALU.mult, op1=ALU.add)
@@ -251,10 +249,11 @@ def tile_attend_gpborrowed_heads_kernel(tc, query, keys_words, keys_scales, gout
 
         times_ds(0, CHUNK)
         nc.vector.tensor_copy(out=h_own[:], in_=hda[:].indirect(first[:]))
-        nc.vector.scalar_tensor_tensor(out=scrap[:], in0=hda[:], scalar=1.0, in1=prob[:], op0=ALU.mult, op1=ALU.mult, accum_out=h_parts[:, 0:1])
+        nc.vector.tensor_tensor(out=scrap[:], in0=hda[:], in1=prob[:], op=ALU.mult)
+        nc.scalar.activation(out=prob[:], in_=scrap[:], func=ACT.Copy, accum_out=h_parts[:, 0:1])
         nc.vector.tensor_tensor(out=h_gap[:], in0=hda[:].indirect(second[:]), in1=h_own[:], op=ALU.subtract)
         times_ds(CHUNK, 2 * CHUNK)
-        nc.vector.scalar_tensor_tensor(out=scrap[:, 0:SLOTS], in0=h_gap[:], scalar=share_over_z[:], in1=p_listed[:], op0=ALU.mult, op1=ALU.mult, accum_out=h_parts[:, 1:2])
+        nc.vector.scalar_tensor_tensor(out=h_own[:], in0=h_gap[:], scalar=share_over_z[:], in1=p_listed[:], op0=ALU.mult, op1=ALU.mult, accum_out=h_parts[:, 1:2])
         times_ds(2 * CHUNK, T)
         nc.vector.tensor_tensor(out=at_first[:].indirect(first[:]), in0=h_gap[:], in1=e1[:], op=ALU.mult)
         neg_parts = sb("neg_parts", 2)

@@ -23,6 +23,7 @@ BANK = 512
 HALVES = T // BANK
 BLOCKS = BANK // P
 CHUNK = 256
+V_PIECES = ((0, 512), (512, 768), (768, 1024))
 PENALTY = 1024.0 * 2.0 * 1024.0
 
 
@@ -157,52 +158,90 @@ def tile_attend_gpborrowed_heads_kernel(tc, query, keys_words, keys_scales, gout
         nc.tensor.transpose(fac_ps[:], fac_rows[:], ident[:])
         fac_cols = sb("fac_cols", T // P)
         nc.scalar.copy(out=fac_cols[:], in_=fac_ps[:, 0 : T // P])
-        v_grouped = [keep.tile([P, BANK, PACK], BF16, name="v_grouped" + str(h), tag="v_grouped" + str(h), align_bytes=64) for h in range(HALVES)]
-        for c in range(T // CHUNK):
-            h, lo = divmod(c * CHUNK, BANK)
-            dst, src = interleave_views(v_grouped[h][:, lo : lo + CHUNK, :], v_raw[c][:])
-            nc.scalar.copy(out=dst, in_=src)
+        v_grouped = [keep.tile([P, hi - lo, PACK], BF16, name="v_grouped" + str(n), tag="v_grouped" + str(n), align_bytes=64)
+                     for n, (lo, hi) in enumerate(V_PIECES)]
+        for n, (lo, hi) in enumerate(V_PIECES):
+            for c in range(lo // CHUNK, hi // CHUNK):
+                dst, src = interleave_views(v_grouped[n][:, c * CHUNK - lo : (c + 1) * CHUNK - lo, :], v_raw[c][:])
+                nc.scalar.copy(out=dst, in_=src)
         c_ps = turned_banks("_c")
         u_ps = banks("u", "")
-        for h in range(HALVES):
-            v_codes, v_scales = quantize("v" + str(h), v_grouped[h][:], BANK)
-            for b in range(BLOCKS):
-                c, i = divmod(h * BLOCKS + b, CHUNK // P)
-                nc.tensor.matmul_mx(out=c_ps[c][:, block_cols(i)], lhsT=v_codes[:, block_cols(b)].bitcast(FP8X4),
-                                    lhsT_scale=v_scales[:, block_cols(b)], rhs=g_codes[:].bitcast(FP8X4), rhs_scale=g_scales[:],
-                                    start=True, stop=True)
         u_turned = keep.tile([P, T], F32, name="u_turned", tag="v_raw3", align_bytes=64)
-        for j in range(T // P):
-            c, i = divmod(j, CHUNK // P)
-            h, b = divmod(j, BLOCKS)
-            nc.scalar.activation(out=u_turned[:, block_cols(j)], in_=c_ps[c][:, block_cols(i)], func=ACT.Copy, scale=fac_cols[:, j : j + 1])
-            nc.tensor.transpose(u_ps[h][:, block_cols(b)], u_turned[:, block_cols(j)], ident[:])
 
+        def weighted_products(n):
+            lo, hi = V_PIECES[n]
+            v_codes, v_scales = quantize("v" + str(n), v_grouped[n][:], hi - lo)
+            for j in range(lo // P, hi // P):
+                c, i = divmod(j, CHUNK // P)
+                here = block_cols(j - lo // P)
+                nc.tensor.matmul_mx(out=c_ps[c][:, block_cols(i)], lhsT=v_codes[:, here].bitcast(FP8X4), lhsT_scale=v_scales[:, here],
+                                    rhs=g_codes[:].bitcast(FP8X4), rhs_scale=g_scales[:], start=True, stop=True)
+            for j in range(lo // P, hi // P):
+                c, i = divmod(j, CHUNK // P)
+                h, b = divmod(j, BLOCKS)
+                nc.scalar.activation(out=u_turned[:, block_cols(j)], in_=c_ps[c][:, block_cols(i)], func=ACT.Copy, scale=fac_cols[:, j : j + 1])
+                nc.tensor.transpose(u_ps[h][:, block_cols(b)], u_turned[:, block_cols(j)], ident[:])
+
+        weighted_products(0)
+        weighted_products(1)
         s = keep.tile([P, T], F32, name="s", tag="v_grouped1", align_bytes=64)
         for h in range(HALVES):
             nc.vector.tensor_tensor(out=s[:, half_cols(h)], in0=a[:, half_cols(h)], in1=at_first[:, half_cols(h)], op=ALU.add)
-        neg_max = sb("neg_max", 1)
+        weighted_products(2)
+        neg_max = keep.tile([P, 1], F32, name="neg_max", tag="v_grouped2", align_bytes=64)
         nc.vector.tensor_reduce(out=neg_max[:], in_=s[:], axis=AXIS_X, op=ALU.max, negate=True)
         p = [keep.tile([P, BANK], F32, name="p" + str(h), tag="p" + str(h), align_bytes=64) for h in range(HALVES)]
         z_parts = [sb("z_part" + str(h), 1) for h in range(HALVES)]
         for h in range(HALVES):
             nc.scalar.activation(out=p[h][:], in_=s[:, half_cols(h)], func=ACT.Exp, bias=neg_max[:], accum_out=z_parts[h][:])
         scrap = sb("scrap", T)
-        up_parts = [sb("up_part" + str(h), 1) for h in range(HALVES)]
+        up_parts = sb("up_parts", 3)
         z = sb("z", 1)
         inv_z = sb("inv_z", 1)
-        nc.vector.scalar_tensor_tensor(out=scrap[:, half_cols(0)], in0=u_ps[0][:], scalar=1.0, in1=p[0][:], op0=ALU.mult, op1=ALU.mult, accum_out=up_parts[0][:])
+
+        def sum_u_p(n):
+            lo, hi = V_PIECES[n]
+            h, at = divmod(lo, BANK)
+            nc.vector.scalar_tensor_tensor(out=scrap[:, lo:hi], in0=u_ps[h][:, at : at + hi - lo], scalar=1.0, in1=p[h][:, at : at + hi - lo],
+                                           op0=ALU.mult, op1=ALU.mult, accum_out=up_parts[:, n : n + 1])
+
+        sum_u_p(0)
         nc.vector.tensor_tensor(out=z[:], in0=z_parts[0][:], in1=z_parts[1][:], op=ALU.add)
+        sum_u_p(1)
         nc.vector.reciprocal(out=inv_z[:], in_=z[:])
-        nc.vector.scalar_tensor_tensor(out=scrap[:, half_cols(1)], in0=u_ps[1][:], scalar=1.0, in1=p[1][:], op0=ALU.mult, op1=ALU.mult, accum_out=up_parts[1][:])
+        sum_u_p(2)
         prob = sb("prob", T)
         for h in range(HALVES):
             nc.scalar.activation(out=prob[:, half_cols(h)], in_=p[h][:], func=ACT.Copy, scale=inv_z[:])
         u_mean = sb("u_mean", 1)
-        nc.vector.tensor_scalar(out=u_mean[:], in0=up_parts[0][:], scalar1=up_parts[1][:], scalar2=inv_z[:], op0=ALU.add, op1=ALU.mult)
+        up_scaled = sb("up_scaled", 3)
+        nc.vector.tensor_scalar(out=up_scaled[:], in0=up_parts[:], scalar1=inv_z[:], scalar2=None, op0=ALU.mult, op1=ALU.add, accum_out=u_mean[:])
         ds = sb("ds", T)
         for h in range(HALVES):
             nc.vector.scalar_tensor_tensor(out=ds[:, half_cols(h)], in0=u_ps[h][:], scalar=u_mean[:], in1=prob[:, half_cols(h)], op0=ALU.subtract, op1=ALU.mult)
+
+        side_turned = turned_banks("_side")
+        moved = keep.tile([P, SLOTS], F32, name="moved", tag="p1", align_bytes=64)
+        nc.scalar.activation(out=moved[:], in_=gap[:], func=ACT.Identity, scale=share_col[:], bias=neg_max[:])
+        listed_staged = sb("listed_staged", SLOTS)
+        prob_ps, p_listed = banks("u", "_side")
+        for c in range(SLOTS // CHUNK):
+            for i in range(CHUNK // P):
+                for k, addend in enumerate((moved, own)):
+                    nc.tensor.matmul(side_turned[c][:, block_cols(i)], lhsT=addend[:, block_cols(2 * c + i)], rhs=ident[:],
+                                     start=k == 0, stop=k == 1, is_transpose=True)
+            nc.scalar.activation(out=listed_staged[:, chunk_cols(c)], in_=side_turned[c][:], func=ACT.Exp)
+        for b in range(BLOCKS):
+            nc.tensor.transpose(p_listed[:, block_cols(b)], listed_staged[:, block_cols(b)], ident[:])
+        prob_staged = keep.tile([P, BANK], F32, name="prob_staged", tag="p1", align_bytes=64)
+        for c in range(BANK // CHUNK):
+            for i in range(CHUNK // P):
+                nc.tensor.transpose(side_turned[2 + c][:, block_cols(i)], prob[:, block_cols(2 * c + i)], ident[:])
+            nc.scalar.copy(out=prob_staged[:, chunk_cols(c)], in_=side_turned[2 + c][:])
+        for b in range(BLOCKS):
+            nc.tensor.transpose(prob_ps[:, block_cols(b)], prob_staged[:, block_cols(b)], ident[:])
+        share_over_z = sb("share_over_z", 1)
+        nc.scalar.activation(out=share_over_z[:], in_=share_col[:], func=ACT.Copy, scale=inv_z[:])
 
         picked = sb("picked", SLOTS)
         nc.vector.tensor_copy(out=picked[:], in_=ds[:].indirect(first[:]))
@@ -214,21 +253,6 @@ def tile_attend_gpborrowed_heads_kernel(tc, query, keys_words, keys_scales, gout
         e1 = sb("e1", SLOTS)
         nc.scalar.activation(out=e1[:], in_=picked[:], func=ACT.Copy, scale=share_col[:])
         partial = turn_back(turned, "_da", PENALTY)
-        moved = keep.tile([P, SLOTS], F32, name="moved", tag="p1", align_bytes=64)
-        nc.scalar.activation(out=moved[:], in_=gap[:], func=ACT.Identity, scale=share_col[:], bias=neg_max[:])
-        listed_turned = psum.tile([P, SLOTS], F32, name="listed_turned", tag="u1")
-        for b in range(BLOCKS):
-            for k, addend in enumerate((moved, own)):
-                nc.tensor.matmul(listed_turned[:, block_cols(b)], lhsT=addend[:, block_cols(b)], rhs=ident[:],
-                                 start=k == 0, stop=k == 1, is_transpose=True)
-        listed_staged = sb("listed_staged", SLOTS)
-        nc.scalar.activation(out=listed_staged[:], in_=listed_turned[:], func=ACT.Exp)
-        p_listed = psum.tile([P, SLOTS], F32, name="p_listed", tag="u0")
-        for b in range(BLOCKS):
-            nc.tensor.transpose(p_listed[:, block_cols(b)], listed_staged[:, block_cols(b)], ident[:])
-        share_over_z = sb("share_over_z", 1)
-        nc.scalar.activation(out=share_over_z[:], in_=share_col[:], func=ACT.Copy, scale=inv_z[:])
-
         hda = sb("hda", T)
         for h in range(HALVES):
             nc.vector.scalar_tensor_tensor(out=hda[:, half_cols(h)], in0=at_first[:, half_cols(h)], scalar=-PENALTY, in1=partial[h][:], op0=ALU.mult, op1=ALU.add)
@@ -240,23 +264,23 @@ def tile_attend_gpborrowed_heads_kernel(tc, query, keys_words, keys_scales, gout
         energy_term = sb("energy_term", T)
         nc.scalar.activation(out=energy_term[:], in_=prob[:], func=ACT.Copy, scale=neg_energy[:])
         hda_ds = sb("hda_ds", T)
-        h_parts = sb("h_parts", 2)
+        for h in range(HALVES):
+            nc.gpsimd.tensor_tensor(out=hda_ds[:, half_cols(h)], in0=hda[:, half_cols(h)], in1=ds[:, half_cols(h)], op=ALU.mult)
+        h_parts = sb("h_parts", 3)
         h_own = sb("h_own", SLOTS)
         h_gap = sb("h_gap", SLOTS)
 
-        def times_ds(lo, hi):
-            nc.vector.tensor_tensor(out=hda_ds[:, lo:hi], in0=hda[:, lo:hi], in1=ds[:, lo:hi], op=ALU.mult)
+        def sum_with_prob(h, prob_half):
+            nc.vector.scalar_tensor_tensor(out=scrap[:, half_cols(h)], in0=prob_half, scalar=1.0, in1=hda[:, half_cols(h)],
+                                           op0=ALU.mult, op1=ALU.mult, accum_out=h_parts[:, h : h + 1])
 
-        times_ds(0, CHUNK)
+        sum_with_prob(0, prob_ps[:])
         nc.vector.tensor_copy(out=h_own[:], in_=hda[:].indirect(first[:]))
-        nc.vector.tensor_tensor(out=scrap[:], in0=hda[:], in1=prob[:], op=ALU.mult)
-        nc.scalar.activation(out=prob[:], in_=scrap[:], func=ACT.Copy, accum_out=h_parts[:, 0:1])
+        sum_with_prob(1, prob[:, half_cols(1)])
         nc.vector.tensor_tensor(out=h_gap[:], in0=hda[:].indirect(second[:]), in1=h_own[:], op=ALU.subtract)
-        times_ds(CHUNK, 2 * CHUNK)
-        nc.vector.scalar_tensor_tensor(out=h_own[:], in0=h_gap[:], scalar=share_over_z[:], in1=p_listed[:], op0=ALU.mult, op1=ALU.mult, accum_out=h_parts[:, 1:2])
-        times_ds(2 * CHUNK, T)
+        nc.vector.scalar_tensor_tensor(out=h_own[:], in0=h_gap[:], scalar=share_over_z[:], in1=p_listed[:], op0=ALU.mult, op1=ALU.mult, accum_out=h_parts[:, 2:3])
         nc.vector.tensor_tensor(out=at_first[:].indirect(first[:]), in0=h_gap[:], in1=e1[:], op=ALU.mult)
-        neg_parts = sb("neg_parts", 2)
+        neg_parts = sb("neg_parts", 3)
         neg_h_mean = sb("neg_h_mean", 1)
         nc.scalar.activation(out=neg_parts[:], in_=h_parts[:], func=ACT.Copy, scale=-1.0, accum_out=neg_h_mean[:])
         mean_term = sb("mean_term", T)

@@ -102,7 +102,7 @@ def tile_attend_gpborrowed_heads_kernel(tc, query, keys_words, keys_scales, gout
         nc.scalar.activation(out=warm[:], in_=at_first[:, 0:1], func=ACT.Exp)
 
         def quantize(name, grouped, cols):
-            codes = sb(name + "_codes", cols, U32)
+            codes = keep.tile([P, cols], U32, name=name + "_codes", tag=name + "_codes", align_bytes=64)
             scales = sb(name + "_scales", cols, U8)
             nc.vector.quantize_mx(out=codes[:].bitcast(FP8X4), scales=scales[:], in_=grouped.rearrange("p c j -> p (c j)"))
             return codes, scales
@@ -113,8 +113,6 @@ def tile_attend_gpborrowed_heads_kernel(tc, query, keys_words, keys_scales, gout
         q_codes, q_scales = quantize("q", q_grouped[:], Q)
         a_ps = turned_banks("_a")
         a = sb("a", T)
-        share_wide = sb("share_wide", SLOTS)
-        nc.vector.tensor_scalar(out=share_wide[:], in0=at_second[:, 0:SLOTS], scalar1=share_col[:], scalar2=None, op0=ALU.add)
         for c in range(T // CHUNK):
             h, lo = divmod(c * CHUNK, BANK)
             nc.tensor.matmul_mx(out=a_ps[c][:], lhsT=q_codes[:].bitcast(FP8X4), lhsT_scale=q_scales[:],
@@ -123,6 +121,8 @@ def tile_attend_gpborrowed_heads_kernel(tc, query, keys_words, keys_scales, gout
                 nc.scalar.copy(out=a[:, chunk_cols(c)], in_=a_ps[c][:])
             else:
                 nc.vector.tensor_copy(out=a[:, chunk_cols(c)], in_=a_ps[c][:])
+        share_wide = keep.tile([P, SLOTS], F32, name="share_wide", tag="q_codes", align_bytes=64)
+        nc.vector.tensor_scalar(out=share_wide[:], in0=at_second[:, 0:SLOTS], scalar1=share_col[:], scalar2=None, op0=ALU.add)
         g_grouped = keep.tile([P, Q, PACK], BF16, name="g_grouped", tag="k_words1", align_bytes=64)
         dst, src = interleave_views(g_grouped[:], g_raw[:])
         nc.scalar.copy(out=dst, in_=src)
@@ -130,11 +130,14 @@ def tile_attend_gpborrowed_heads_kernel(tc, query, keys_words, keys_scales, gout
         own = sb("own", SLOTS)
         gap = sb("gap", SLOTS)
 
-        def turn_into(dst_banks, addend, opens, closes):
-            for j in range(T // P):
-                c, i = divmod(j, CHUNK // P)
-                nc.tensor.matmul(dst_banks[c][:, block_cols(i)], lhsT=addend[:, block_cols(j)], rhs=ident[:],
+        def turn_chunk(bank, addend, opens, closes):
+            for i in range(CHUNK // P):
+                nc.tensor.matmul(bank[:, block_cols(i)], lhsT=addend[:, block_cols(i)], rhs=ident[:],
                                  start=opens and i == 0, stop=closes and i == CHUNK // P - 1, is_transpose=True)
+
+        def turn_into(dst_banks, addend, opens, closes):
+            for c in range(T // CHUNK):
+                turn_chunk(dst_banks[c], addend[:, chunk_cols(c)], opens, closes)
 
         def turn_back(src_banks, use, scale):
             back = banks("back", use)
@@ -226,18 +229,16 @@ def tile_attend_gpborrowed_heads_kernel(tc, query, keys_words, keys_scales, gout
         listed_staged = sb("listed_staged", SLOTS)
         prob_ps, p_listed = banks("u", "_side")
         for c in range(SLOTS // CHUNK):
-            for i in range(CHUNK // P):
-                for k, addend in enumerate((moved, own)):
-                    nc.tensor.matmul(side_turned[c][:, block_cols(i)], lhsT=addend[:, block_cols(2 * c + i)], rhs=ident[:],
-                                     start=k == 0, stop=k == 1, is_transpose=True)
-            nc.scalar.activation(out=listed_staged[:, chunk_cols(c)], in_=side_turned[c][:], func=ACT.Exp)
+            turn_chunk(side_turned[2 + c], own[:, chunk_cols(c)], True, False)
+            turn_chunk(side_turned[2 + c], moved[:, chunk_cols(c)], False, True)
+            nc.scalar.activation(out=listed_staged[:, chunk_cols(c)], in_=side_turned[2 + c][:], func=ACT.Exp)
         for b in range(BLOCKS):
             nc.tensor.transpose(p_listed[:, block_cols(b)], listed_staged[:, block_cols(b)], ident[:])
         prob_staged = keep.tile([P, BANK], F32, name="prob_staged", tag="p1", align_bytes=64)
         for c in range(BANK // CHUNK):
             for i in range(CHUNK // P):
-                nc.tensor.transpose(side_turned[2 + c][:, block_cols(i)], prob[:, block_cols(2 * c + i)], ident[:])
-            nc.scalar.copy(out=prob_staged[:, chunk_cols(c)], in_=side_turned[2 + c][:])
+                nc.tensor.transpose(side_turned[c][:, block_cols(i)], prob[:, block_cols(2 * c + i)], ident[:])
+            nc.scalar.copy(out=prob_staged[:, chunk_cols(c)], in_=side_turned[c][:])
         for b in range(BLOCKS):
             nc.tensor.transpose(prob_ps[:, block_cols(b)], prob_staged[:, block_cols(b)], ident[:])
         share_over_z = sb("share_over_z", 1)
@@ -264,8 +265,8 @@ def tile_attend_gpborrowed_heads_kernel(tc, query, keys_words, keys_scales, gout
         energy_term = sb("energy_term", T)
         nc.scalar.activation(out=energy_term[:], in_=prob[:], func=ACT.Copy, scale=neg_energy[:])
         hda_ds = sb("hda_ds", T)
-        for h in range(HALVES):
-            nc.gpsimd.tensor_tensor(out=hda_ds[:, half_cols(h)], in0=hda[:, half_cols(h)], in1=ds[:, half_cols(h)], op=ALU.mult)
+        for lo, hi in V_PIECES[0:2]:
+            nc.gpsimd.tensor_tensor(out=hda_ds[:, lo:hi], in0=hda[:, lo:hi], in1=ds[:, lo:hi], op=ALU.mult)
         h_parts = sb("h_parts", 3)
         h_own = sb("h_own", SLOTS)
         h_gap = sb("h_gap", SLOTS)
@@ -278,6 +279,7 @@ def tile_attend_gpborrowed_heads_kernel(tc, query, keys_words, keys_scales, gout
         nc.vector.tensor_copy(out=h_own[:], in_=hda[:].indirect(first[:]))
         sum_with_prob(1, prob[:, half_cols(1)])
         nc.vector.tensor_tensor(out=h_gap[:], in0=hda[:].indirect(second[:]), in1=h_own[:], op=ALU.subtract)
+        nc.vector.tensor_tensor(out=hda_ds[:, chunk_cols(3)], in0=hda[:, chunk_cols(3)], in1=ds[:, chunk_cols(3)], op=ALU.mult)
         nc.vector.scalar_tensor_tensor(out=h_own[:], in0=h_gap[:], scalar=share_over_z[:], in1=p_listed[:], op0=ALU.mult, op1=ALU.mult, accum_out=h_parts[:, 2:3])
         nc.vector.tensor_tensor(out=at_first[:].indirect(first[:]), in0=h_gap[:], in1=e1[:], op=ALU.mult)
         neg_parts = sb("neg_parts", 3)
@@ -287,8 +289,10 @@ def tile_attend_gpborrowed_heads_kernel(tc, query, keys_words, keys_scales, gout
         for c in range(T // CHUNK):
             nc.scalar.activation(out=mean_term[:, chunk_cols(c)], in_=ds[:, chunk_cols(c)], func=ACT.Copy, scale=neg_h_mean[:])
         turned = turned_banks("_hs")
-        turn_into(turned, energy_term, True, False)
-        turn_into(turned, hda_ds, False, False)
+        for c in range(T // CHUNK):
+            early, late = (energy_term, hda_ds) if c == 3 else (hda_ds, energy_term)
+            turn_chunk(turned[c], early[:, chunk_cols(c)], True, False)
+            turn_chunk(turned[c], late[:, chunk_cols(c)], False, False)
         turn_into(turned, mean_term, False, True)
         partial = turn_back(turned, "_hs", 1.0)
         hs = sb("hs", T)

from contextlib import ExitStack

import concourse.mybir as mybir
from concourse.masks import make_identity

D, E, T, Q, SLOTS = 512, 512, 1024, 128, 512
FLOPS = 2 * D * Q * T + 2 * E * Q * T

F32 = mybir.dt.float32
BF16 = mybir.dt.bfloat16
I32 = mybir.dt.int32
U32 = mybir.dt.uint32
U16 = mybir.dt.uint16
U8 = mybir.dt.uint8
FP8X4 = mybir.dt.float8_e4m3fn_x4
ALU = mybir.AluOpType
ACT = mybir.ActivationFunctionType
AXIS_X = mybir.AxisListType.X

P = 128
PACK = 4
BANK = 512
HALVES = T // BANK
BLOCKS = BANK // P
CHUNK = 256
V_PIECES = ((0, 512), (512, 768), (768, 1024))
PENALTY = 1024.0 * 2.0 * 1024.0


def half_cols(h):
    return slice(h * BANK, (h + 1) * BANK)


def chunk_cols(c):
    return slice(c * CHUNK, (c + 1) * CHUNK)


def block_cols(b):
    return slice(b * P, (b + 1) * P)


def interleave_views(grouped, raw):
    return (grouped.rearrange("p (c i) j -> p c j i", i=4), raw.rearrange("p j (c i) -> p c j i", i=4))


def tile_attend_gpborrowed_heads_kernel(tc, query, keys_words, keys_scales, gout, vals, share, fac, base, offs, offs2, out):
    nc = tc.nc
    with ExitStack() as ctx:
        keep = ctx.enter_context(tc.tile_pool(name="keep", bufs=1))
        psum = ctx.enter_context(tc.psum_pool(name="psum", bufs=1))

        def sb(name, cols, dtype=F32):
            return keep.tile([P, cols], dtype, name=name, align_bytes=64)

        def banks(tag, use):
            return [psum.tile([P, BANK], F32, name=tag + str(h) + use, tag=tag + str(h)) for h in range(HALVES)]

        def turned_banks(use):
            return [psum.tile([P, CHUNK], F32, name="turned" + str(c) + use, tag="turned" + str(c)) for c in range(T // CHUNK)]

        k_scales = sb("k_scales", T, U8)
        nc.gpsimd.memset(k_scales[:].bitcast(I32), 0)
        fac_rows = sb("fac_rows", P)
        nc.gpsimd.memset(fac_rows[:], 0.0)
        ident = sb("ident", P)
        make_identity(nc, ident[:])
        at_first = sb("at_first", T)
        at_second = sb("at_second", T)
        nc.vector.memset(at_first[:], 0.0)
        nc.vector.memset(at_second[:], 0.0)

        q_raw = keep.tile([P, PACK, Q], F32, name="q_raw")
        nc.sync.dma_start(out=q_raw[:], in_=query.rearrange("(p j) q -> p j q", j=PACK))
        for quad in range(4):
            nc.scalar.dma_start(out=k_scales[32 * quad : 32 * quad + 4, :].bitcast(I32),
                                in_=keys_scales[0, 4 * quad : 4 * quad + 4, :].bitcast(I32))
        words = keys_words[0].rearrange("p n t -> p (n t)").bitcast(I32)
        k_words = []
        for h in range(HALVES):
            k_half = keep.tile([P, BANK], I32, name="k_words" + str(h), tag="k_words" + str(h), align_bytes=64)
            nc.sync.dma_start(out=k_half[:], in_=words[:, half_cols(h)])
            k_words.append(k_half)
        share_col = sb("share_col", 1)
        nc.sync.dma_start(out=share_col[:], in_=share)
        first = keep.tile([P, SLOTS // 16], U16, name="first")
        nc.sync.dma_start(first[:], offs)
        second = keep.tile([P, SLOTS // 16], U16, name="second")
        nc.sync.dma_start(second[:], offs2)
        nc.sync.dma_start(out=fac_rows[0 : T // P, :], in_=fac.rearrange("o (j p) -> (o j) p", p=P))
        g_raw = keep.tile([P, PACK, Q], F32, name="g_raw")
        nc.sync.dma_start(out=g_raw[:], in_=gout.rearrange("(p j) q -> p j q", j=PACK))
        v_rows = vals.rearrange("(p j) t -> p j t", j=PACK)
        v_raw = []
        for c in range(T // CHUNK):
            raw = keep.tile([P, PACK, CHUNK], F32, name="v_raw" + str(c), tag="v_raw" + str(c), align_bytes=64)
            nc.sync.dma_start(out=raw[:], in_=v_rows[:, :, c * CHUNK : (c + 1) * CHUNK])
            v_raw.append(raw)
        base_sb = sb("base_sb", T)
        nc.sync.dma_start(out=base_sb[:], in_=base)

        warm = sb("warm", 1)
        nc.scalar.activation(out=warm[:], in_=at_first[:, 0:1], func=ACT.Exp)

        def quantize(name, grouped, cols):
            codes = keep.tile([P, cols], U32, name=name + "_codes", tag=name + "_codes", align_bytes=64)
            scales = sb(name + "_scales", cols, U8)
            nc.vector.quantize_mx(out=codes[:].bitcast(FP8X4), scales=scales[:], in_=grouped.rearrange("p c j -> p (c j)"))
            return codes, scales

        q_grouped = keep.tile([P, Q, PACK], BF16, name="q_grouped", align_bytes=64)
        dst, src = interleave_views(q_grouped[:], q_raw[:])
        nc.vector.tensor_copy(out=dst, in_=src)
        q_codes, q_scales = quantize("q", q_grouped[:], Q)
        a_ps = turned_banks("_a")
        a = sb("a", T)
        for c in range(T // CHUNK):
            h, lo = divmod(c * CHUNK, BANK)
            nc.tensor.matmul_mx(out=a_ps[c][:], lhsT=q_codes[:].bitcast(FP8X4), lhsT_scale=q_scales[:],
                                rhs=k_words[h][:, lo : lo + CHUNK].bitcast(FP8X4), rhs_scale=k_scales[:, chunk_cols(c)], start=True, stop=True)
            if c % 2 == 0:
                nc.scalar.copy(out=a[:, chunk_cols(c)], in_=a_ps[c][:])
            else:
                nc.vector.tensor_copy(out=a[:, chunk_cols(c)], in_=a_ps[c][:])
        share_wide = keep.tile([P, SLOTS], F32, name="share_wide", tag="q_codes", align_bytes=64)
        nc.vector.tensor_scalar(out=share_wide[:], in0=at_second[:, 0:SLOTS], scalar1=share_col[:], scalar2=None, op0=ALU.add)
        g_grouped = keep.tile([P, Q, PACK], BF16, name="g_grouped", tag="k_words1", align_bytes=64)
        dst, src = interleave_views(g_grouped[:], g_raw[:])
        nc.scalar.copy(out=dst, in_=src)

        own = sb("own", SLOTS)
        gap = sb("gap", SLOTS)

        def turn_chunk(bank, addend, opens, closes):
            for i in range(CHUNK // P):
                nc.tensor.matmul(bank[:, block_cols(i)], lhsT=addend[:, block_cols(i)], rhs=ident[:],
                                 start=opens and i == 0, stop=closes and i == CHUNK // P - 1, is_transpose=True)

        def turn_into(dst_banks, addend, opens, closes):
            for c in range(T // CHUNK):
                turn_chunk(dst_banks[c], addend[:, chunk_cols(c)], opens, closes)

        def turn_back(src_banks, use, scale):
            back = banks("back", use)
            for c in range(T // CHUNK):
                staged = sb("staged" + str(c) + use, CHUNK)
                nc.scalar.activation(out=staged[:], in_=src_banks[c][:], func=ACT.Copy, scale=scale)
                for i in range(CHUNK // P):
                    h, b = divmod(c * (CHUNK // P) + i, BLOCKS)
                    nc.tensor.transpose(back[h][:, block_cols(b)], staged[:, block_cols(i)], ident[:])
            return back

        for part in range(2):
            nc.vector.tensor_copy(out=own[:, 256 * part : 256 * part + 256], in_=a[:].indirect(first[:, 16 * part : 16 * part + 16]))
        for part in range(2):
            nc.vector.tensor_tensor(out=gap[:, 256 * part : 256 * part + 256], in0=a[:].indirect(second[:, 16 * part : 16 * part + 16]),
                                    in1=own[:, 256 * part : 256 * part + 256], op=ALU.subtract)
        g_codes, g_scales = quantize("g", g_grouped[:], Q)
        nc.vector.tensor_tensor(out=at_first[:].indirect(first[:]), in0=gap[:], in1=share_wide[:], op=ALU.mult)

        fac_ps = psum.tile([P, P], F32, name="fac_ps", tag="u0")
        nc.tensor.transpose(fac_ps[:], fac_rows[:], ident[:])
        fac_cols = sb("fac_cols", T // P)
        nc.scalar.copy(out=fac_cols[:], in_=fac_ps[:, 0 : T // P])
        v_grouped = [keep.tile([P, hi - lo, PACK], BF16, name="v_grouped" + str(n), tag="v_grouped" + str(n), align_bytes=64)
                     for n, (lo, hi) in enumerate(V_PIECES)]
        for n, (lo, hi) in enumerate(V_PIECES):
            for c in range(lo // CHUNK, hi // CHUNK):
                dst, src = interleave_views(v_grouped[n][:, c * CHUNK - lo : (c + 1) * CHUNK - lo, :], v_raw[c][:])
                nc.scalar.copy(out=dst, in_=src)
        c_ps = turned_banks("_c")
        u_ps = banks("u", "")
        u_turned = keep.tile([P, T], F32, name="u_turned", tag="v_raw3", align_bytes=64)

        def weighted_products(n):
            lo, hi = V_PIECES[n]
            v_codes, v_scales = quantize("v" + str(n), v_grouped[n][:], hi - lo)
            for j in range(lo // P, hi // P):
                c, i = divmod(j, CHUNK // P)
                here = block_cols(j - lo // P)
                nc.tensor.matmul_mx(out=c_ps[c][:, block_cols(i)], lhsT=v_codes[:, here].bitcast(FP8X4), lhsT_scale=v_scales[:, here],
                                    rhs=g_codes[:].bitcast(FP8X4), rhs_scale=g_scales[:], start=True, stop=True)
            for j in range(lo // P, hi // P):
                c, i = divmod(j, CHUNK // P)
                h, b = divmod(j, BLOCKS)
                nc.scalar.activation(out=u_turned[:, block_cols(j)], in_=c_ps[c][:, block_cols(i)], func=ACT.Copy, scale=fac_cols[:, j : j + 1])
                nc.tensor.transpose(u_ps[h][:, block_cols(b)], u_turned[:, block_cols(j)], ident[:])

        weighted_products(0)
        weighted_products(1)
        s = keep.tile([P, T], F32, name="s", tag="v_grouped1", align_bytes=64)
        for h in range(HALVES):
            nc.vector.tensor_tensor(out=s[:, half_cols(h)], in0=a[:, half_cols(h)], in1=at_first[:, half_cols(h)], op=ALU.add)
        weighted_products(2)
        neg_max = keep.tile([P, 1], F32, name="neg_max", tag="v_grouped2", align_bytes=64)
        nc.vector.tensor_reduce(out=neg_max[:], in_=s[:], axis=AXIS_X, op=ALU.max, negate=True)
        p = [keep.tile([P, BANK], F32, name="p" + str(h), tag="p" + str(h), align_bytes=64) for h in range(HALVES)]
        z_parts = [sb("z_part" + str(h), 1) for h in range(HALVES)]
        for h in range(HALVES):
            nc.scalar.activation(out=p[h][:], in_=s[:, half_cols(h)], func=ACT.Exp, bias=neg_max[:], accum_out=z_parts[h][:])
        scrap = sb("scrap", T)
        up_parts = sb("up_parts", 3)
        z = sb("z", 1)
        inv_z = sb("inv_z", 1)

        def sum_u_p(n):
            lo, hi = V_PIECES[n]
            h, at = divmod(lo, BANK)
            nc.vector.scalar_tensor_tensor(out=scrap[:, lo:hi], in0=u_ps[h][:, at : at + hi - lo], scalar=1.0, in1=p[h][:, at : at + hi - lo],
                                           op0=ALU.mult, op1=ALU.mult, accum_out=up_parts[:, n : n + 1])

        sum_u_p(0)
        nc.vector.tensor_tensor(out=z[:], in0=z_parts[0][:], in1=z_parts[1][:], op=ALU.add)
        sum_u_p(1)
        nc.vector.reciprocal(out=inv_z[:], in_=z[:])
        sum_u_p(2)
        prob = sb("prob", T)
        for h in range(HALVES):
            nc.scalar.activation(out=prob[:, half_cols(h)], in_=p[h][:], func=ACT.Copy, scale=inv_z[:])
        u_mean = sb("u_mean", 1)
        up_scaled = sb("up_scaled", 3)
        nc.vector.tensor_scalar(out=up_scaled[:], in0=up_parts[:], scalar1=inv_z[:], scalar2=None, op0=ALU.mult, op1=ALU.add, accum_out=u_mean[:])
        ds = sb("ds", T)
        for h in range(HALVES):
            nc.vector.scalar_tensor_tensor(out=ds[:, half_cols(h)], in0=u_ps[h][:], scalar=u_mean[:], in1=prob[:, half_cols(h)], op0=ALU.subtract, op1=ALU.mult)

        side_turned = turned_banks("_side")
        moved = keep.tile([P, SLOTS], F32, name="moved", tag="p1", align_bytes=64)
        nc.scalar.activation(out=moved[:], in_=gap[:], func=ACT.Identity, scale=share_col[:], bias=neg_max[:])
        listed_staged = sb("listed_staged", SLOTS)
        prob_ps, p_listed = banks("u", "_side")
        for c in range(SLOTS // CHUNK):
            turn_chunk(side_turned[2 + c], own[:, chunk_cols(c)], True, False)
            turn_chunk(side_turned[2 + c], moved[:, chunk_cols(c)], False, True)
            nc.scalar.activation(out=listed_staged[:, chunk_cols(c)], in_=side_turned[2 + c][:], func=ACT.Exp)
        for b in range(BLOCKS):
            nc.tensor.transpose(p_listed[:, block_cols(b)], listed_staged[:, block_cols(b)], ident[:])
        prob_staged = keep.tile([P, BANK], F32, name="prob_staged", tag="p1", align_bytes=64)
        for c in range(BANK // CHUNK):
            for i in range(CHUNK // P):
                nc.tensor.transpose(side_turned[c][:, block_cols(i)], prob[:, block_cols(2 * c + i)], ident[:])
            nc.scalar.copy(out=prob_staged[:, chunk_cols(c)], in_=side_turned[c][:])
        for b in range(BLOCKS):
            nc.tensor.transpose(prob_ps[:, block_cols(b)], prob_staged[:, block_cols(b)], ident[:])
        share_over_z = sb("share_over_z", 1)
        nc.scalar.activation(out=share_over_z[:], in_=share_col[:], func=ACT.Copy, scale=inv_z[:])

        picked = sb("picked", SLOTS)
        nc.vector.tensor_copy(out=picked[:], in_=ds[:].indirect(first[:]))
        turned = turned_banks("_da")
        turn_into(turned, ds, True, False)
        nc.vector.tensor_tensor(out=at_second[:].indirect(second[:]), in0=picked[:], in1=share_wide[:], op=ALU.mult)
        turn_into(turned, at_second, False, True)
        nc.vector.tensor_tensor(out=at_first[:].indirect(first[:]), in0=picked[:], in1=share_wide[:], op=ALU.mult)
        e1 = sb("e1", SLOTS)
        nc.scalar.activation(out=e1[:], in_=picked[:], func=ACT.Copy, scale=share_col[:])
        partial = turn_back(turned, "_da", PENALTY)
        hda = sb("hda", T)
        for h in range(HALVES):
            nc.vector.scalar_tensor_tensor(out=hda[:, half_cols(h)], in0=at_first[:, half_cols(h)], scalar=-PENALTY, in1=partial[h][:], op0=ALU.mult, op1=ALU.add)

        squares = sb("squares", 1)
        nc.scalar.activation(out=s[:], in_=hda[:], func=ACT.Square, accum_out=squares[:])
        neg_energy = sb("neg_energy", 1)
        nc.scalar.activation(out=neg_energy[:], in_=squares[:], func=ACT.Copy, scale=-1.0 / PENALTY)
        energy_term = sb("energy_term", T)
        nc.scalar.activation(out=energy_term[:], in_=prob[:], func=ACT.Copy, scale=neg_energy[:])
        hda_ds = sb("hda_ds", T)
        for lo, hi in V_PIECES[0:2]:
            nc.gpsimd.tensor_tensor(out=hda_ds[:, lo:hi], in0=hda[:, lo:hi], in1=ds[:, lo:hi], op=ALU.mult)
        h_parts = sb("h_parts", 3)
        h_own = sb("h_own", SLOTS)
        h_gap = sb("h_gap", SLOTS)

        def sum_with_prob(h, prob_half):
            nc.vector.scalar_tensor_tensor(out=scrap[:, half_cols(h)], in0=prob_half, scalar=1.0, in1=hda[:, half_cols(h)],
                                           op0=ALU.mult, op1=ALU.mult, accum_out=h_parts[:, h : h + 1])

        sum_with_prob(0, prob_ps[:])
        nc.vector.tensor_copy(out=h_own[:], in_=hda[:].indirect(first[:]))
        sum_with_prob(1, prob[:, half_cols(1)])
        nc.vector.tensor_tensor(out=h_gap[:], in0=hda[:].indirect(second[:]), in1=h_own[:], op=ALU.subtract)
        nc.vector.tensor_tensor(out=hda_ds[:, chunk_cols(3)], in0=hda[:, chunk_cols(3)], in1=ds[:, chunk_cols(3)], op=ALU.mult)
        nc.vector.scalar_tensor_tensor(out=h_own[:], in0=h_gap[:], scalar=share_over_z[:], in1=p_listed[:], op0=ALU.mult, op1=ALU.mult, accum_out=h_parts[:, 2:3])
        nc.vector.tensor_tensor(out=at_first[:].indirect(first[:]), in0=h_gap[:], in1=e1[:], op=ALU.mult)
        neg_parts = sb("neg_parts", 3)
        neg_h_mean = sb("neg_h_mean", 1)
        nc.scalar.activation(out=neg_parts[:], in_=h_parts[:], func=ACT.Copy, scale=-1.0, accum_out=neg_h_mean[:])
        mean_term = sb("mean_term", T)
        for c in range(T // CHUNK):
            nc.scalar.activation(out=mean_term[:, chunk_cols(c)], in_=ds[:, chunk_cols(c)], func=ACT.Copy, scale=neg_h_mean[:])
        turned = turned_banks("_hs")
        for c in range(T // CHUNK):
            early, late = (energy_term, hda_ds) if c == 3 else (hda_ds, energy_term)
            turn_chunk(turned[c], early[:, chunk_cols(c)], True, False)
            turn_chunk(turned[c], late[:, chunk_cols(c)], False, False)
        turn_into(turned, mean_term, False, True)
        partial = turn_back(turned, "_hs", 1.0)
        hs = sb("hs", T)
        for h in range(HALVES):
            nc.vector.tensor_tensor(out=hs[:, half_cols(h)], in0=partial[h][:], in1=at_first[:, half_cols(h)], op=ALU.add)

        turned = turned_banks("_out")
        nc.vector.tensor_copy(out=picked[:], in_=hs[:].indirect(first[:]))
        turn_into(turned, hs, True, False)
        turn_into(turned, base_sb, False, False)
        nc.vector.tensor_tensor(out=at_second[:].indirect(second[:]), in0=picked[:], in1=share_wide[:], op=ALU.mult)
        turn_into(turned, at_second, False, True)
        nc.vector.tensor_tensor(out=at_first[:].indirect(first[:]), in0=picked[:], in1=share_wide[:], op=ALU.mult)
        partial = turn_back(turned, "_out", 1.0)
        for c in range(T // CHUNK):
            h, lo = divmod(c * CHUNK, BANK)
            result = sb("result" + str(c), CHUNK)
            nc.vector.tensor_tensor(out=result[:], in0=partial[h][:, lo : lo + CHUNK], in1=at_first[:, chunk_cols(c)], op=ALU.subtract)
            queue = nc.sync if c % 2 == 0 else nc.scalar
            queue.dma_start(out=out[:, chunk_cols(c)], in_=result[:])
